import numpy as np, ml_dtypes
CORES = [17,81,89,18,82,90]
N = 6
GR, GC, HH, WW = 2, 3, 16, 16
def setup_inputs(rng):
    return {"x": rng.standard_normal((N, 128, HH * WW), dtype=np.float32).astype(ml_dtypes.bfloat16), "w": rng.standard_normal((N, 128, 9 * 128), dtype=np.float32).astype(ml_dtypes.bfloat16)}
def setup_inputs_big(rng):
    d = setup_inputs(rng)
    for k in ("x", "w"): d[k] = (d[k].astype(np.float32) * 1024.0).astype(d[k].dtype)
    return d
def setup_inputs_small(rng):
    d = setup_inputs(rng)
    for k in ("x", "w"): d[k] = (d[k].astype(np.float32) * (1 / 1024.0)).astype(d[k].dtype)
    return d
def setup_inputs_apart(rng):
    d = setup_inputs(rng)
    f = (10.0 ** rng.permutation(np.linspace(-1.5, 1.5, N))).astype(np.float32).reshape(N, 1, 1)
    for k in ("x", "w"): d[k] = (d[k].astype(np.float32) * f).astype(d[k].dtype)
    return d
def reference(x, w):
    X = x.astype(np.float64).reshape(GR, GC, 128, HH, WW); W = w.astype(np.float64)
    g = np.concatenate([np.concatenate(list(X[i]), axis=2) for i in range(GR)], axis=1)
    y = np.zeros((N, 128, HH * WW))
    for r in range(N):
        i0, j0 = HH * (r // GC), WW * (r % GC)
        for a in range(3):
            for b in range(3):
                sh = np.roll(g, (-2 * (a - 1), -2 * (b - 1)), axis=(1, 2))[:, i0:i0 + HH, j0:j0 + WW]
                y[r] += W[r][:, 128 * (3 * a + b):128 * (3 * a + b) + 128].T @ sh.reshape(128, HH * WW)
    return {"y": y.astype(ml_dtypes.bfloat16 if x.dtype != np.float64 else np.float64)}

@@ -1,0 +1,159 @@
+from concourse.bass import DstId, RemoteDMATransfer
+from concourse.mybir import AluOpType
+
+GR, GC = 2, 3
+
+SCRATCH = {
+    "xs": ("sbuf", [128, 8, 2, 16], "bfloat16"),
+    "wsb": ("sbuf", [128, 1152], "bfloat16"),
+    "vb": ("sbuf", [128, 2, 2, 16], "bfloat16"),
+    "cb": ("sbuf", [128, 2, 10, 2, 2], "bfloat16"),
+    "sb": ("sbuf", [128, 2, 20, 2, 2], "bfloat16"),
+    "h": ("sbuf", [128, 2, 10, 2, 2], "bfloat16"),
+    "te": ("sbuf", [128, 16, 2, 2], "float32"),
+    "ysb": ("sbuf", [128, 16, 8, 2], "bfloat16"),
+    "p0": ("psum", [128, 32, 8, 2], "float32"),
+    "pe": ("psum", [128, 128, 2, 2], "float32"),
+}
+SEMAPHORES = ["sx", "sw0", "sw1", "sw2", "sp", "sc", "sv", "sl", "sr", "sloc", "sm0", "sm1", "sf", "sy"]
+
+
+def _engines(mask):
+    return [e for e in range(mask.bit_length()) if (mask >> e) & 1]
+
+
+def _bits(es):
+    m = 0
+    for e in es:
+        m |= 1 << e
+    return m
+
+
+def rank_program(g, core, T, topo):
+    rank = T.rank_of(core)
+    if rank is None:
+        return
+    cores = T.cores
+    S = T.sem
+    row, col = divmod(rank, GC)
+
+    def column(k):
+        return [cores[r * GC + (k % GC)] for r in range(GR)]
+
+    def relay_of(k):
+        dests = column(k - 1) + column(k + 1)
+        return [m for m in column(k) if all(topo.may_write(m, d) for d in dests)][-1]
+
+    def dst_id(c):
+        rid, pid, _ = topo.addr(c)
+        return DstId(rid=rid, pnc=pid)
+
+    def links(src, dst):
+        a, b = topo.chip(src), topo.chip(dst)
+        if a == b:
+            return 0
+        if topo.mates(a, b):
+            return 1
+        if topo.same_plane(a, b):
+            return 2
+        return 3
+
+    other = column(col)[1 - row]
+    relay = relay_of(col)
+    is_relay = core == relay
+    edge_col = (0, 14)
+
+    g.sync.dma_start(T.xs[:], T.x[:]).then_inc(S.sx, 16)
+    for a in (1, 0, 2):
+        g.scalar.dma_start(T.wsb[:, 384 * a:384 * a + 384], T.w[:, 384 * a:384 * a + 384]).then_inc(S["sw%d" % a], 16)
+
+    g.vector.wait_ge(S.sx, 16)
+    for s in range(2):
+        c = edge_col[s]
+        if is_relay:
+            g.vector.tensor_copy(out=T.sb[:, s, 12:20, :, :], in_=T.xs[:, :, :, c:c + 2]).then_inc(S.sp, 1)
+            g.vector.tensor_copy(out=T.sb[:, s, 0:2, :, :], in_=T.xs[:, 0:8:7, :, c:c + 2]).then_inc(S.sp, 1)
+        else:
+            g.vector.tensor_copy(out=T.cb[:, s, 0:8, :, :], in_=T.xs[:, :, :, c:c + 2]).then_inc(S.sp, 1)
+            g.vector.tensor_copy(out=T.cb[:, s, 8:10, :, :], in_=T.xs[:, 0:8:7, :, c:c + 2]).then_inc(S.sp, 1)
+
+    def rows_to_other(es):
+        n = len(es) // 2
+        return [RemoteDMATransfer(dst_ids=[dst_id(other)], dma_engine_mask=_bits(es[k * n:(k + 1) * n]),
+                                  remote_sem=S.sv, src=T.xs[:, 7 * k, :, :], dst=T.vb[:, k, :, :]) for k in range(2)]
+
+    if is_relay:
+        left, right = column(col - 1), column(col + 1)
+        common = topo.mask(core, other)
+        for d in left + right:
+            common &= topo.mask(core, d)
+        es = _engines(common)[:8]
+        g.wait_ge(S.sx, 16)
+        g.remote_dma_fused(rows_to_other(es), local_sem=S.sloc)
+        g.wait_ge(S.sp, 4)
+        g.wait_ge(S.sc, 8)
+        trs = []
+        for s in range(2):
+            for q in range(GR):
+                half = 1 if q == row else 0
+                k = len(trs)
+                trs.append(RemoteDMATransfer(
+                    dst_ids=[dst_id((left, right)[s][q])], dma_engine_mask=_bits(es[2 * k:2 * k + 2]),
+                    remote_sem=(S.sr, S.sl)[s],
+                    src=T.sb[:, s, 10 * half:10 * half + 10, :, :], dst=T.h[:, 1 - s, :, :, :]))
+        g.remote_dma_fused(trs, local_sem=S.sloc)
+        g.wait_ge(S.sloc, 16)
+    else:
+        es = _engines(topo.mask(core, relay))[:8]
+        g.wait_ge(S.sp, 4)
+        g.remote_dma_fused([RemoteDMATransfer(dst_ids=[dst_id(relay)], dma_engine_mask=_bits(es[4 * s:4 * s + 4]),
+                                              remote_sem=S.sc, src=T.cb[:, s, :, :, :], dst=T.sb[:, s, 2:12, :, :])
+                            for s in range(2)], local_sem=S.sloc)
+        g.wait_ge(S.sx, 16)
+        g.remote_dma_fused(rows_to_other(es), local_sem=S.sloc)
+        g.wait_ge(S.sloc, 16)
+
+    def wt(a, b):
+        t = 3 * a + b
+        return T.wsb[:, 128 * t:128 * t + 128]
+
+    out_q = ((1, 8), (0, 8), (0, 7))
+    in_c = ((0, 14), (0, 16), (2, 16))
+    g.tensor.wait_ge(S.sx, 16)
+    first = True
+    for a in (1, 0, 2):
+        g.tensor.wait_ge(S["sw%d" % a], 16)
+        r0, r1 = ((2, 16), (0, 16), (0, 14))[a]
+        p0, p1 = ((0, 7), (0, 8), (1, 8))[a]
+        for b in (1, 0, 2):
+            g.tensor.matmul(out=T.p0[:, r0:r1, out_q[b][0]:out_q[b][1], :], lhsT=wt(a, b),
+                            rhs=T.xs[:, p0:p1, :, in_c[b][0]:in_c[b][1]], start=first, stop=False).then_inc(S.sm0, 1)
+            first = False
+    g.tensor.wait_ge(S.sv, 8)
+    for a in (0, 2):
+        r0 = 0 if a == 0 else 14
+        k = 1 if a == 0 else 0
+        for b in range(3):
+            g.tensor.matmul(out=T.p0[:, r0:r0 + 2, out_q[b][0]:out_q[b][1], :], lhsT=wt(a, b),
+                            rhs=T.vb[:, k, :, in_c[b][0]:in_c[b][1]], start=False,
+                            stop=(a == 2 and b == 2)).then_inc(S.sm0, 1)
+    sides = sorted(range(2), key=lambda s: links(relay_of(col - 1 + 2 * s), core))
+    for s in sides:
+        g.tensor.wait_ge((S.sl, S.sr)[s], 2)
+        b = 2 * s
+        pieces = ((0, 0, 16, 1, 9), (1, 0, 16, 2, 10), (2, 0, 14, 3, 10), (2, 14, 16, 0, 1))
+        for n, (a, r0, r1, p0, p1) in enumerate(pieces):
+            g.tensor.matmul(out=T.pe[:, r0:r1, s, :], lhsT=wt(a, b), rhs=T.h[:, s, p0:p1, :, :],
+                            start=(n == 0), stop=(n == 3)).then_inc(S.sm1, 1)
+
+    g.vector.wait_ge(S.sm0, 15)
+    g.vector.tensor_copy(out=T.te[:], in_=T.p0[:, 0:16, 0:8:7, :]).then_inc(S.sf, 1)
+    g.vector.tensor_copy(out=T.ysb[:, :, 1:7, :], in_=T.p0[:, 0:16, 1:7, :]).then_inc(S.sf, 1)
+    g.vector.wait_ge(S.sf, 2)
+    g.vector.wait_ge(S.sm1, 8)
+    g.vector.tensor_tensor(out=T.ysb[:, :, 0:8:7, :], in0=T.pe[:, 0:16, :, :], in1=T.te[:],
+                           op=AluOpType.add).then_inc(S.sf, 1)
+
+    g.sync.wait_ge(S.sf, 3)
+    g.sync.dma_start(T.y[:], T.ysb[:]).then_inc(S.sy, 16)
+    g.sync.wait_ge(S.sy, 16)

@@ -7,15 +7,21 @@ SCRATCH = {
     "xs": ("sbuf", [128, 8, 2, 16], "bfloat16"),
     "wsb": ("sbuf", [128, 1152], "bfloat16"),
     "vb": ("sbuf", [128, 2, 2, 16], "bfloat16"),
-    "cb": ("sbuf", [128, 2, 10, 2, 2], "bfloat16"),
-    "sb": ("sbuf", [128, 2, 20, 2, 2], "bfloat16"),
+    "cb": ("sbuf", [128, 20, 2, 2], "bfloat16"),
+    "sb": ("sbuf", [128, 36, 2, 2], "bfloat16"),
+    "rc": ("sbuf", [128, 2, 2, 2, 2], "bfloat16"),
     "h": ("sbuf", [128, 2, 10, 2, 2], "bfloat16"),
+    "hc": ("sbuf", [128, 2, 2, 2, 2], "bfloat16"),
     "te": ("sbuf", [128, 16, 2, 2], "float32"),
     "ysb": ("sbuf", [128, 16, 8, 2], "bfloat16"),
     "p0": ("psum", [128, 32, 8, 2], "float32"),
     "pe": ("psum", [128, 128, 2, 2], "float32"),
 }
-SEMAPHORES = ["sx", "sw0", "sw1", "sw2", "sp", "sc", "sv", "sl", "sr", "sloc", "sm0", "sm1", "sf", "sy"]
+SEMAPHORES = ["sx", "sw0", "sw1", "sw2", "sp", "sc", "sv", "sk", "sl", "sr", "sloc", "sm0", "sm1", "sf", "sy"]
+
+NV_RELAY = 8
+NV_FEEDER = 4
+NB_FEEDER = 8
 
 
 def _engines(mask):
@@ -44,6 +50,9 @@ def rank_program(g, core, T, topo):
         dests = column(k - 1) + column(k + 1)
         return [m for m in column(k) if all(topo.may_write(m, d) for d in dests)][-1]
 
+    def feeder_row(k):
+        return 1 - column(k).index(relay_of(k))
+
     def dst_id(c):
         rid, pid, _ = topo.addr(c)
         return DstId(rid=rid, pnc=pid)
@@ -70,12 +79,13 @@ def rank_program(g, core, T, topo):
     g.vector.wait_ge(S.sx, 16)
     for s in range(2):
         c = edge_col[s]
+        four, sixteen = T.xs[:, 0:8:7, :, c:c + 2], T.xs[:, :, :, c:c + 2]
         if is_relay:
-            g.vector.tensor_copy(out=T.sb[:, s, 12:20, :, :], in_=T.xs[:, :, :, c:c + 2]).then_inc(S.sp, 1)
-            g.vector.tensor_copy(out=T.sb[:, s, 0:2, :, :], in_=T.xs[:, 0:8:7, :, c:c + 2]).then_inc(S.sp, 1)
+            g.vector.tensor_copy(out=T.rc[:, s, :, :, :], in_=four).then_inc(S.sp, 1)
+            g.vector.tensor_copy(out=T.sb[:, 28 * s:28 * s + 8, :, :], in_=sixteen).then_inc(S.sp, 1)
         else:
-            g.vector.tensor_copy(out=T.cb[:, s, 0:8, :, :], in_=T.xs[:, :, :, c:c + 2]).then_inc(S.sp, 1)
-            g.vector.tensor_copy(out=T.cb[:, s, 8:10, :, :], in_=T.xs[:, 0:8:7, :, c:c + 2]).then_inc(S.sp, 1)
+            g.vector.tensor_copy(out=T.cb[:, 18 * s:18 * s + 2, :, :], in_=four).then_inc(S.sp, 1)
+            g.vector.tensor_copy(out=T.cb[:, 2 + 8 * s:10 + 8 * s, :, :], in_=sixteen).then_inc(S.sp, 1)
 
     def rows_to_other(es):
         n = len(es) // 2
@@ -83,74 +93,95 @@ def rank_program(g, core, T, topo):
                                   remote_sem=S.sv, src=T.xs[:, 7 * k, :, :], dst=T.vb[:, k, :, :]) for k in range(2)]
 
     if is_relay:
-        left, right = column(col - 1), column(col + 1)
+        nbr = (column(col - 1), column(col + 1))
         common = topo.mask(core, other)
-        for d in left + right:
+        for d in nbr[0] + nbr[1]:
             common &= topo.mask(core, d)
-        es = _engines(common)[:8]
+        es = _engines(common)[:NV_RELAY]
         g.wait_ge(S.sx, 16)
         g.remote_dma_fused(rows_to_other(es), local_sem=S.sloc)
         g.wait_ge(S.sp, 4)
-        g.wait_ge(S.sc, 8)
+        g.remote_dma_fused([RemoteDMATransfer(dst_ids=[dst_id(nbr[s][1 - row])], dma_engine_mask=_bits(es[4 * s:4 * s + 4]),
+                                              remote_sem=S.sk, src=T.rc[:, s, :, :, :], dst=T.hc[:, 1 - s, :, :, :])
+                            for s in range(2)], local_sem=S.sloc)
+        g.wait_ge(S.sc, NB_FEEDER)
+        first_pair = ((8, 0), (18, 26))
         trs = []
         for s in range(2):
             for q in range(GR):
-                half = 1 if q == row else 0
+                p = first_pair[s][1 if q == row else 0]
                 k = len(trs)
                 trs.append(RemoteDMATransfer(
-                    dst_ids=[dst_id((left, right)[s][q])], dma_engine_mask=_bits(es[2 * k:2 * k + 2]),
-                    remote_sem=(S.sr, S.sl)[s],
-                    src=T.sb[:, s, 10 * half:10 * half + 10, :, :], dst=T.h[:, 1 - s, :, :, :]))
+                    dst_ids=[dst_id(nbr[s][q])], dma_engine_mask=_bits(es[2 * k:2 * k + 2]),
+                    remote_sem=(S.sr, S.sl)[s], src=T.sb[:, p:p + 10, :, :], dst=T.h[:, 1 - s, :, :, :]))
         g.remote_dma_fused(trs, local_sem=S.sloc)
-        g.wait_ge(S.sloc, 16)
+        g.wait_ge(S.sloc, NV_RELAY + 8 + 8)
     else:
-        es = _engines(topo.mask(core, relay))[:8]
-        g.wait_ge(S.sp, 4)
-        g.remote_dma_fused([RemoteDMATransfer(dst_ids=[dst_id(relay)], dma_engine_mask=_bits(es[4 * s:4 * s + 4]),
-                                              remote_sem=S.sc, src=T.cb[:, s, :, :, :], dst=T.sb[:, s, 2:12, :, :])
-                            for s in range(2)], local_sem=S.sloc)
+        es = _engines(topo.mask(core, relay))
         g.wait_ge(S.sx, 16)
-        g.remote_dma_fused(rows_to_other(es), local_sem=S.sloc)
-        g.wait_ge(S.sloc, 16)
+        g.remote_dma_fused(rows_to_other(es[NB_FEEDER:NB_FEEDER + NV_FEEDER]), local_sem=S.sloc)
+        g.wait_ge(S.sp, 4)
+        g.remote_dma_fused([RemoteDMATransfer(dst_ids=[dst_id(relay)], dma_engine_mask=_bits(es[:NB_FEEDER]),
+                                              remote_sem=S.sc, src=T.cb[:], dst=T.sb[:, 8:28, :, :])],
+                           local_sem=S.sloc)
+        g.wait_ge(S.sloc, NV_FEEDER + NB_FEEDER)
 
     def wt(a, b):
         t = 3 * a + b
         return T.wsb[:, 128 * t:128 * t + 128]
 
+    ahead = [row == feeder_row(col - 1 + 2 * s) for s in range(2)]
+    n_ahead = sum(1 for s in range(2) if ahead[s])
+    n0 = 15 + 2 * n_ahead
+    done = [0]
+
+    def mm0(out, lhsT, rhs):
+        done[0] += 1
+        g.tensor.matmul(out=out, lhsT=lhsT, rhs=rhs, start=(done[0] == 1), stop=(done[0] == n0)).then_inc(S.sm0, 1)
+
     out_q = ((1, 8), (0, 8), (0, 7))
     in_c = ((0, 14), (0, 16), (2, 16))
     g.tensor.wait_ge(S.sx, 16)
-    first = True
     for a in (1, 0, 2):
         g.tensor.wait_ge(S["sw%d" % a], 16)
         r0, r1 = ((2, 16), (0, 16), (0, 14))[a]
         p0, p1 = ((0, 7), (0, 8), (1, 8))[a]
         for b in (1, 0, 2):
-            g.tensor.matmul(out=T.p0[:, r0:r1, out_q[b][0]:out_q[b][1], :], lhsT=wt(a, b),
-                            rhs=T.xs[:, p0:p1, :, in_c[b][0]:in_c[b][1]], start=first, stop=False).then_inc(S.sm0, 1)
-            first = False
-    g.tensor.wait_ge(S.sv, 8)
+            mm0(T.p0[:, r0:r1, out_q[b][0]:out_q[b][1], :], wt(a, b), T.xs[:, p0:p1, :, in_c[b][0]:in_c[b][1]])
+    g.tensor.wait_ge(S.sv, NV_FEEDER if is_relay else NV_RELAY)
     for a in (0, 2):
         r0 = 0 if a == 0 else 14
         k = 1 if a == 0 else 0
         for b in range(3):
-            g.tensor.matmul(out=T.p0[:, r0:r0 + 2, out_q[b][0]:out_q[b][1], :], lhsT=wt(a, b),
-                            rhs=T.vb[:, k, :, in_c[b][0]:in_c[b][1]], start=False,
-                            stop=(a == 2 and b == 2)).then_inc(S.sm0, 1)
-    sides = sorted(range(2), key=lambda s: links(relay_of(col - 1 + 2 * s), core))
-    for s in sides:
+            mm0(T.p0[:, r0:r0 + 2, out_q[b][0]:out_q[b][1], :], wt(a, b), T.vb[:, k, :, in_c[b][0]:in_c[b][1]])
+    if n_ahead:
+        g.tensor.wait_ge(S.sk, 4 * n_ahead)
+        for s in range(2):
+            if ahead[s]:
+                mm0(T.p0[:, 0:2, 7 * s, :], wt(0, 2 * s), T.hc[:, s, 1, :, :])
+                mm0(T.p0[:, 14:16, 7 * s, :], wt(2, 2 * s), T.hc[:, s, 0, :, :])
+
+    n1 = 0
+    for s in sorted(range(2), key=lambda s: links(relay_of(col - 1 + 2 * s), core)):
         g.tensor.wait_ge((S.sl, S.sr)[s], 2)
         b = 2 * s
-        pieces = ((0, 0, 16, 1, 9), (1, 0, 16, 2, 10), (2, 0, 14, 3, 10), (2, 14, 16, 0, 1))
+        if ahead[s]:
+            G = 2 if s == 1 else 0
+            pieces = ((1, 0, 16, G, G + 8), (0, 2, 16, G, G + 7), (2, 0, 14, G + 1, G + 8))
+        elif s == 1:
+            pieces = ((1, 0, 16, 0, 8), (2, 0, 16, 1, 9), (0, 2, 16, 0, 7), (0, 0, 2, 9, 10))
+        else:
+            pieces = ((1, 0, 16, 2, 10), (0, 0, 16, 1, 9), (2, 0, 14, 3, 10), (2, 14, 16, 0, 1))
         for n, (a, r0, r1, p0, p1) in enumerate(pieces):
             g.tensor.matmul(out=T.pe[:, r0:r1, s, :], lhsT=wt(a, b), rhs=T.h[:, s, p0:p1, :, :],
-                            start=(n == 0), stop=(n == 3)).then_inc(S.sm1, 1)
+                            start=(n == 0), stop=(n == len(pieces) - 1)).then_inc(S.sm1, 1)
+        n1 += len(pieces)
 
-    g.vector.wait_ge(S.sm0, 15)
+    g.vector.wait_ge(S.sm0, n0)
     g.vector.tensor_copy(out=T.te[:], in_=T.p0[:, 0:16, 0:8:7, :]).then_inc(S.sf, 1)
     g.vector.tensor_copy(out=T.ysb[:, :, 1:7, :], in_=T.p0[:, 0:16, 1:7, :]).then_inc(S.sf, 1)
     g.vector.wait_ge(S.sf, 2)
-    g.vector.wait_ge(S.sm1, 8)
+    g.vector.wait_ge(S.sm1, n1)
     g.vector.tensor_tensor(out=T.ysb[:, :, 0:8:7, :], in0=T.pe[:, 0:16, :, :], in1=T.te[:],
                            op=AluOpType.add).then_inc(S.sf, 1)
 

@@ -1,5 +1,5 @@
 from concourse.bass import DstId, RemoteDMATransfer
-from concourse.mybir import AluOpType
+from concourse.mybir import AluOpType, ActivationFunctionType
 
 GR, GC = 2, 3
 
@@ -7,21 +7,25 @@ SCRATCH = {
     "xs": ("sbuf", [128, 8, 2, 16], "bfloat16"),
     "wsb": ("sbuf", [128, 1152], "bfloat16"),
     "vb": ("sbuf", [128, 2, 2, 16], "bfloat16"),
-    "cb": ("sbuf", [128, 20, 2, 2], "bfloat16"),
-    "sb": ("sbuf", [128, 36, 2, 2], "bfloat16"),
-    "rc": ("sbuf", [128, 2, 2, 2, 2], "bfloat16"),
-    "h": ("sbuf", [128, 2, 10, 2, 2], "bfloat16"),
-    "hc": ("sbuf", [128, 2, 2, 2, 2], "bfloat16"),
+    "eb": ("sbuf", [128, 2, 8, 2, 2], "bfloat16"),
+    "cb": ("sbuf", [128, 16, 2, 2], "bfloat16"),
+    "c4": ("sbuf", [128, 4, 2, 2], "bfloat16"),
+    "sb": ("sbuf", [128, 20, 2, 2], "bfloat16"),
+    "s4": ("sbuf", [128, 4, 2, 2], "bfloat16"),
+    "hA": ("sbuf", [128, 2, 10, 2, 2], "bfloat16"),
+    "hD": ("sbuf", [128, 2, 2, 8, 2, 2], "bfloat16"),
+    "hB": ("sbuf", [128, 2, 2, 2, 2], "bfloat16"),
     "te": ("sbuf", [128, 16, 2, 2], "float32"),
     "ysb": ("sbuf", [128, 16, 8, 2], "bfloat16"),
     "p0": ("psum", [128, 32, 8, 2], "float32"),
-    "pe": ("psum", [128, 128, 2, 2], "float32"),
+    "pe0": ("psum", [128, 256, 2], "float32"),
+    "pe1": ("psum", [128, 256, 2], "float32"),
 }
-SEMAPHORES = ["sx", "sw0", "sw1", "sw2", "sp", "sc", "sv", "sk", "sl", "sr", "sloc", "sm0", "sm1", "sf", "sy"]
+SEMAPHORES = ["sx", "sw0", "sw1", "sw2", "sgb", "sg4", "sge", "sgr", "sc", "sc4", "sv", "sE0", "sE1", "sL0", "sL1",
+              "sloc", "sm0", "sme0", "sme1", "sf", "sy"]
 
-NV_RELAY = 8
-NV_FEEDER = 4
-NB_FEEDER = 8
+NV = 4
+NO = 8
 
 
 def _engines(mask):
@@ -46,12 +50,13 @@ def rank_program(g, core, T, topo):
     def column(k):
         return [cores[r * GC + (k % GC)] for r in range(GR)]
 
-    def relay_of(k):
-        dests = column(k - 1) + column(k + 1)
-        return [m for m in column(k) if all(topo.may_write(m, d) for d in dests)][-1]
+    def relay_of(k, s):
+        dests = column(k - 1 + 2 * s)
+        cap = [m for m in column(k) if all(topo.may_write(m, d) for d in dests)]
+        return None if len(cap) == GR else cap[-1]
 
-    def feeder_row(k):
-        return 1 - column(k).index(relay_of(k))
+    def n_relayed(k):
+        return sum(1 for s in range(2) if relay_of(k, s) is not None)
 
     def dst_id(c):
         rid, pid, _ = topo.addr(c)
@@ -68,71 +73,93 @@ def rank_program(g, core, T, topo):
         return 3
 
     other = column(col)[1 - row]
-    relay = relay_of(col)
-    is_relay = core == relay
+    nbr = (column(col - 1), column(col + 1))
+    role = []
+    for s in range(2):
+        rel = relay_of(col, s)
+        role.append("direct" if rel is None else ("relay" if rel == core else "feeder"))
+    fs = [s for s in range(2) if role[s] == "feeder"]
+    rs = [s for s in range(2) if role[s] == "relay"]
+    ds = [s for s in range(2) if role[s] == "direct"]
     edge_col = (0, 14)
 
     g.sync.dma_start(T.xs[:], T.x[:]).then_inc(S.sx, 16)
     for a in (1, 0, 2):
-        g.scalar.dma_start(T.wsb[:, 384 * a:384 * a + 384], T.w[:, 384 * a:384 * a + 384]).then_inc(S["sw%d" % a], 16)
+        g.sync.dma_start(T.wsb[:, 384 * a:384 * a + 384], T.w[:, 384 * a:384 * a + 384]).then_inc(S["sw%d" % a], 16)
 
+    def sixteen(s):
+        return T.xs[:, :, :, edge_col[s]:edge_col[s] + 2]
+
+    def four(s):
+        return T.xs[:, 0:8:7, :, edge_col[s]:edge_col[s] + 2]
+
+    jobs = []
+    for s in fs:
+        jobs.append((T.cb[:, 8 * s:8 * s + 8, :, :], sixteen(s), S.sgb))
+    for s in fs:
+        jobs.append((T.c4[:, 2 * s:2 * s + 2, :, :], four(s), S.sg4))
+    for s in rs + ds:
+        jobs.append((T.eb[:, s, :, :, :], sixteen(s), S.sge))
+    for s in rs:
+        jobs.append((T.sb[:, 18 * s:18 * s + 2, :, :], four(s), S.sgr))
     g.vector.wait_ge(S.sx, 16)
-    for s in range(2):
-        c = edge_col[s]
-        four, sixteen = T.xs[:, 0:8:7, :, c:c + 2], T.xs[:, :, :, c:c + 2]
-        if is_relay:
-            g.vector.tensor_copy(out=T.rc[:, s, :, :, :], in_=four).then_inc(S.sp, 1)
-            g.vector.tensor_copy(out=T.sb[:, 28 * s:28 * s + 8, :, :], in_=sixteen).then_inc(S.sp, 1)
+    g.scalar.wait_ge(S.sx, 16)
+    for n, (o, i, sem) in enumerate(jobs):
+        if n % 2 == 0:
+            g.vector.tensor_copy(out=o, in_=i).then_inc(sem, 1)
         else:
-            g.vector.tensor_copy(out=T.cb[:, 18 * s:18 * s + 2, :, :], in_=four).then_inc(S.sp, 1)
-            g.vector.tensor_copy(out=T.cb[:, 2 + 8 * s:10 + 8 * s, :, :], in_=sixteen).then_inc(S.sp, 1)
+            g.scalar.activation(out=o, in_=i, func=ActivationFunctionType.Copy).then_inc(sem, 1)
 
-    def rows_to_other(es):
-        n = len(es) // 2
-        return [RemoteDMATransfer(dst_ids=[dst_id(other)], dma_engine_mask=_bits(es[k * n:(k + 1) * n]),
-                                  remote_sem=S.sv, src=T.xs[:, 7 * k, :, :], dst=T.vb[:, k, :, :]) for k in range(2)]
+    far_mask = topo.mask(core, other)
+    for d in cores:
+        if topo.chip(d) != topo.chip(core):
+            far_mask &= topo.mask(core, d)
+    es = _engines(far_mask)[:NO]
+    es_on = [e for e in _engines(topo.mask(core, other)) if e not in es]
+    sent = [0]
 
-    if is_relay:
-        nbr = (column(col - 1), column(col + 1))
-        common = topo.mask(core, other)
-        for d in nbr[0] + nbr[1]:
-            common &= topo.mask(core, d)
-        es = _engines(common)[:NV_RELAY]
-        g.wait_ge(S.sx, 16)
-        g.remote_dma_fused(rows_to_other(es), local_sem=S.sloc)
-        g.wait_ge(S.sp, 4)
-        g.remote_dma_fused([RemoteDMATransfer(dst_ids=[dst_id(nbr[s][1 - row])], dma_engine_mask=_bits(es[4 * s:4 * s + 4]),
-                                              remote_sem=S.sk, src=T.rc[:, s, :, :, :], dst=T.hc[:, 1 - s, :, :, :])
-                            for s in range(2)], local_sem=S.sloc)
-        g.wait_ge(S.sc, NB_FEEDER)
-        first_pair = ((8, 0), (18, 26))
-        trs = []
-        for s in range(2):
-            for q in range(GR):
-                p = first_pair[s][1 if q == row else 0]
-                k = len(trs)
-                trs.append(RemoteDMATransfer(
-                    dst_ids=[dst_id(nbr[s][q])], dma_engine_mask=_bits(es[2 * k:2 * k + 2]),
-                    remote_sem=(S.sr, S.sl)[s], src=T.sb[:, p:p + 10, :, :], dst=T.h[:, 1 - s, :, :, :]))
-        g.remote_dma_fused(trs, local_sem=S.sloc)
-        g.wait_ge(S.sloc, NV_RELAY + 8 + 8)
-    else:
-        es = _engines(topo.mask(core, relay))
-        g.wait_ge(S.sx, 16)
-        g.remote_dma_fused(rows_to_other(es[NB_FEEDER:NB_FEEDER + NV_FEEDER]), local_sem=S.sloc)
-        g.wait_ge(S.sp, 4)
-        g.remote_dma_fused([RemoteDMATransfer(dst_ids=[dst_id(relay)], dma_engine_mask=_bits(es[:NB_FEEDER]),
-                                              remote_sem=S.sc, src=T.cb[:], dst=T.sb[:, 8:28, :, :])],
-                           local_sem=S.sloc)
-        g.wait_ge(S.sloc, NV_FEEDER + NB_FEEDER)
+    def call(items):
+        n = NO // len(items)
+        g.remote_dma_fused([RemoteDMATransfer(dst_ids=[dst_id(d)], dma_engine_mask=_bits(es[k * n:(k + 1) * n]),
+                                              remote_sem=sem, src=a, dst=b)
+                            for k, (d, sem, a, b) in enumerate(items)], local_sem=S.sloc)
+        sent[0] += n * len(items)
+
+    SE, SL = (S.sE0, S.sE1), (S.sL0, S.sL1)
+    g.wait_ge(S.sx, 16)
+    nv = NV // 2
+    g.remote_dma_fused([RemoteDMATransfer(dst_ids=[dst_id(other)], dma_engine_mask=_bits(es_on[k * nv:(k + 1) * nv]),
+                                          remote_sem=S.sv, src=T.xs[:, 7 * k, :, :], dst=T.vb[:, k, :, :])
+                        for k in range(2)], local_sem=S.sloc)
+    sent[0] += NV
+    if fs:
+        lo, hi = 8 * min(fs), 8 * max(fs) + 8
+        g.wait_ge(S.sgb, len(fs))
+        call([(other, S.sc, T.cb[:, lo:hi, :, :], T.sb[:, 2 + lo:2 + hi, :, :])])
+        lo, hi = 2 * min(fs), 2 * max(fs) + 2
+        g.wait_ge(S.sg4, len(fs))
+        call([(other, S.sc4, T.c4[:, lo:hi, :, :], T.s4[:, lo:hi, :, :])])
+    if rs or ds:
+        g.wait_ge(S.sge, len(rs) + len(ds))
+    if rs:
+        call([(nbr[s][row], SE[1 - s], T.eb[:, s, :, :, :], T.hD[:, 1 - s, 0, :, :, :]) for s in rs])
+    for s in ds:
+        call([(nbr[s][q], SE[1 - s], T.eb[:, s, :, :, :], T.hD[:, 1 - s, 0 if q == row else 1, :, :, :])
+              for q in range(GR)])
+    if rs:
+        g.wait_ge(S.sgr, len(rs))
+        g.wait_ge(S.sc, NO)
+        call([(nbr[s][1 - row], SL[1 - s], T.sb[:, 10 * s:10 * s + 10, :, :], T.hA[:, 1 - s, :, :, :]) for s in rs])
+        g.wait_ge(S.sc4, NO)
+        for s in sorted(rs, key=lambda s: -links(core, nbr[s][row])):
+            call([(nbr[s][row], SL[1 - s], T.s4[:, 2 * s:2 * s + 2, :, :], T.hB[:, 1 - s, :, :, :])])
+    g.wait_ge(S.sloc, sent[0])
 
     def wt(a, b):
         t = 3 * a + b
         return T.wsb[:, 128 * t:128 * t + 128]
 
-    ahead = [row == feeder_row(col - 1 + 2 * s) for s in range(2)]
-    n_ahead = sum(1 for s in range(2) if ahead[s])
-    n0 = 15 + 2 * n_ahead
+    n0 = 15
     done = [0]
 
     def mm0(out, lhsT, rhs):
@@ -148,43 +175,54 @@ def rank_program(g, core, T, topo):
         p0, p1 = ((0, 7), (0, 8), (1, 8))[a]
         for b in (1, 0, 2):
             mm0(T.p0[:, r0:r1, out_q[b][0]:out_q[b][1], :], wt(a, b), T.xs[:, p0:p1, :, in_c[b][0]:in_c[b][1]])
-    g.tensor.wait_ge(S.sv, NV_FEEDER if is_relay else NV_RELAY)
+    g.tensor.wait_ge(S.sv, NV)
     for a in (0, 2):
         r0 = 0 if a == 0 else 14
         k = 1 if a == 0 else 0
         for b in range(3):
             mm0(T.p0[:, r0:r0 + 2, out_q[b][0]:out_q[b][1], :], wt(a, b), T.vb[:, k, :, in_c[b][0]:in_c[b][1]])
-    if n_ahead:
-        g.tensor.wait_ge(S.sk, 4 * n_ahead)
-        for s in range(2):
-            if ahead[s]:
-                mm0(T.p0[:, 0:2, 7 * s, :], wt(0, 2 * s), T.hc[:, s, 1, :, :])
-                mm0(T.p0[:, 14:16, 7 * s, :], wt(2, 2 * s), T.hc[:, s, 0, :, :])
 
-    n1 = 0
-    for s in sorted(range(2), key=lambda s: links(relay_of(col - 1 + 2 * s), core)):
-        g.tensor.wait_ge((S.sl, S.sr)[s], 2)
-        b = 2 * s
-        if ahead[s]:
-            G = 2 if s == 1 else 0
-            pieces = ((1, 0, 16, G, G + 8), (0, 2, 16, G, G + 7), (2, 0, 14, G + 1, G + 8))
-        elif s == 1:
-            pieces = ((1, 0, 16, 0, 8), (2, 0, 16, 1, 9), (0, 2, 16, 0, 7), (0, 0, 2, 9, 10))
+    P16 = ((1, 0, 16, 0, 8), (0, 2, 16, 0, 7), (2, 0, 14, 1, 8))
+    P4_OF_16 = ((0, 0, 2, 7, 8), (2, 14, 16, 0, 1))
+    P4 = ((0, 0, 2, 1, 2), (2, 14, 16, 0, 1))
+    PA = (((1, 0, 16, 0, 8), (2, 0, 16, 1, 9), (0, 2, 16, 0, 7), (0, 0, 2, 9, 10)),
+          ((1, 0, 16, 2, 10), (0, 0, 16, 1, 9), (2, 0, 14, 3, 10), (2, 14, 16, 0, 1)))
+    PE, SME = (T.pe0, T.pe1), (S.sme0, S.sme1)
+    early, late, total = [], [], [0, 0]
+    for s in range(2):
+        k = col - 1 + 2 * s
+        rel = relay_of(k, 1 - s)
+        if rel is None:
+            early.append((0, s, SE[s], NO, [(T.hD[:, s, 0, :, :, :], P16), (T.hD[:, s, 1, :, :, :], P4_OF_16)]))
+            total[s] = 5
+        elif column(k).index(rel) == row:
+            early.append((1, s, SE[s], NO // n_relayed(k), [(T.hD[:, s, 0, :, :, :], P16)]))
+            late.append(((1, n_relayed(k), links(rel, core)), s, SL[s], NO, [(T.hB[:, s, :, :, :], P4)]))
+            total[s] = 5
         else:
-            pieces = ((1, 0, 16, 2, 10), (0, 0, 16, 1, 9), (2, 0, 14, 3, 10), (2, 14, 16, 0, 1))
-        for n, (a, r0, r1, p0, p1) in enumerate(pieces):
-            g.tensor.matmul(out=T.pe[:, r0:r1, s, :], lhsT=wt(a, b), rhs=T.h[:, s, p0:p1, :, :],
-                            start=(n == 0), stop=(n == len(pieces) - 1)).then_inc(S.sm1, 1)
-        n1 += len(pieces)
+            late.append(((0, n_relayed(k), links(rel, core)), s, SL[s], NO // n_relayed(k), [(T.hA[:, s, :, :, :], PA[s])]))
+            total[s] = 4
+    count = [0, 0]
+    order = []
+    for _, s, sem, cnt, parts in sorted(early, key=lambda e: e[0]) + sorted(late, key=lambda e: e[0]):
+        g.tensor.wait_ge(sem, cnt)
+        for buf, pieces in parts:
+            for a, r0, r1, p0, p1 in pieces:
+                count[s] += 1
+                g.tensor.matmul(out=PE[s][:, r0:r1, :], lhsT=wt(a, 2 * s), rhs=buf[:, p0:p1, :, :],
+                                start=(count[s] == 1), stop=(count[s] == total[s])).then_inc(SME[s], 1)
+        if count[s] == total[s]:
+            order.append(s)
 
     g.vector.wait_ge(S.sm0, n0)
     g.vector.tensor_copy(out=T.te[:], in_=T.p0[:, 0:16, 0:8:7, :]).then_inc(S.sf, 1)
     g.vector.tensor_copy(out=T.ysb[:, :, 1:7, :], in_=T.p0[:, 0:16, 1:7, :]).then_inc(S.sf, 1)
     g.vector.wait_ge(S.sf, 2)
-    g.vector.wait_ge(S.sm1, n1)
-    g.vector.tensor_tensor(out=T.ysb[:, :, 0:8:7, :], in0=T.pe[:, 0:16, :, :], in1=T.te[:],
-                           op=AluOpType.add).then_inc(S.sf, 1)
+    for s in order:
+        g.vector.wait_ge(SME[s], total[s])
+        g.vector.tensor_tensor(out=T.ysb[:, :, 7 * s, :], in0=PE[s][:, 0:16, :], in1=T.te[:, :, s, :],
+                               op=AluOpType.add).then_inc(S.sf, 1)
 
-    g.sync.wait_ge(S.sf, 3)
+    g.sync.wait_ge(S.sf, 4)
     g.sync.dma_start(T.y[:], T.ysb[:]).then_inc(S.sy, 16)
     g.sync.wait_ge(S.sy, 16)

from concourse.bass import DstId, RemoteDMATransfer
from concourse.mybir import AluOpType, ActivationFunctionType

GR, GC = 2, 3

SCRATCH = {
    "xs": ("sbuf", [128, 8, 2, 16], "bfloat16"),
    "wsb": ("sbuf", [128, 1152], "bfloat16"),
    "vb": ("sbuf", [128, 2, 2, 16], "bfloat16"),
    "eb": ("sbuf", [128, 2, 8, 2, 2], "bfloat16"),
    "cb": ("sbuf", [128, 16, 2, 2], "bfloat16"),
    "c4": ("sbuf", [128, 4, 2, 2], "bfloat16"),
    "sb": ("sbuf", [128, 20, 2, 2], "bfloat16"),
    "s4": ("sbuf", [128, 4, 2, 2], "bfloat16"),
    "hA": ("sbuf", [128, 2, 10, 2, 2], "bfloat16"),
    "hD": ("sbuf", [128, 2, 2, 8, 2, 2], "bfloat16"),
    "hB": ("sbuf", [128, 2, 2, 2, 2], "bfloat16"),
    "te": ("sbuf", [128, 16, 2, 2], "float32"),
    "ysb": ("sbuf", [128, 16, 8, 2], "bfloat16"),
    "p0": ("psum", [128, 32, 8, 2], "float32"),
    "pe0": ("psum", [128, 256, 2], "float32"),
    "pe1": ("psum", [128, 256, 2], "float32"),
}
SEMAPHORES = ["sx", "sw0", "sw1", "sw2", "sgb", "sg4", "sge", "sgr", "sc", "sc4", "sv", "sE0", "sE1", "sL0", "sL1",
              "sloc", "sm0", "sme0", "sme1", "sf", "sy"]

NV = 4
NO = 8


def _engines(mask):
    return [e for e in range(mask.bit_length()) if (mask >> e) & 1]


def _bits(es):
    m = 0
    for e in es:
        m |= 1 << e
    return m


def rank_program(g, core, T, topo):
    rank = T.rank_of(core)
    if rank is None:
        return
    cores = T.cores
    S = T.sem
    row, col = divmod(rank, GC)

    def column(k):
        return [cores[r * GC + (k % GC)] for r in range(GR)]

    def relay_of(k, s):
        dests = column(k - 1 + 2 * s)
        cap = [m for m in column(k) if all(topo.may_write(m, d) for d in dests)]
        return None if len(cap) == GR else cap[-1]

    def n_relayed(k):
        return sum(1 for s in range(2) if relay_of(k, s) is not None)

    def dst_id(c):
        rid, pid, _ = topo.addr(c)
        return DstId(rid=rid, pnc=pid)

    def links(src, dst):
        a, b = topo.chip(src), topo.chip(dst)
        if a == b:
            return 0
        if topo.mates(a, b):
            return 1
        if topo.same_plane(a, b):
            return 2
        return 3

    other = column(col)[1 - row]
    nbr = (column(col - 1), column(col + 1))
    role = []
    for s in range(2):
        rel = relay_of(col, s)
        role.append("direct" if rel is None else ("relay" if rel == core else "feeder"))
    fs = [s for s in range(2) if role[s] == "feeder"]
    rs = [s for s in range(2) if role[s] == "relay"]
    ds = [s for s in range(2) if role[s] == "direct"]
    edge_col = (0, 14)

    g.sync.dma_start(T.xs[:], T.x[:]).then_inc(S.sx, 16)
    for a in (1, 0, 2):
        g.sync.dma_start(T.wsb[:, 384 * a:384 * a + 384], T.w[:, 384 * a:384 * a + 384]).then_inc(S["sw%d" % a], 16)

    def sixteen(s):
        return T.xs[:, :, :, edge_col[s]:edge_col[s] + 2]

    def four(s):
        return T.xs[:, 0:8:7, :, edge_col[s]:edge_col[s] + 2]

    jobs = []
    for s in fs:
        jobs.append((T.cb[:, 8 * s:8 * s + 8, :, :], sixteen(s), S.sgb))
    for s in fs:
        jobs.append((T.c4[:, 2 * s:2 * s + 2, :, :], four(s), S.sg4))
    for s in rs + ds:
        jobs.append((T.eb[:, s, :, :, :], sixteen(s), S.sge))
    for s in rs:
        jobs.append((T.sb[:, 18 * s:18 * s + 2, :, :], four(s), S.sgr))
    g.vector.wait_ge(S.sx, 16)
    g.scalar.wait_ge(S.sx, 16)
    for n, (o, i, sem) in enumerate(jobs):
        if n % 2 == 0:
            g.vector.tensor_copy(out=o, in_=i).then_inc(sem, 1)
        else:
            g.scalar.activation(out=o, in_=i, func=ActivationFunctionType.Copy).then_inc(sem, 1)

    far_mask = topo.mask(core, other)
    for d in cores:
        if topo.chip(d) != topo.chip(core):
            far_mask &= topo.mask(core, d)
    es = _engines(far_mask)[:NO]
    es_on = [e for e in _engines(topo.mask(core, other)) if e not in es]
    sent = [0]

    def call(items):
        n = NO // len(items)
        g.remote_dma_fused([RemoteDMATransfer(dst_ids=[dst_id(d)], dma_engine_mask=_bits(es[k * n:(k + 1) * n]),
                                              remote_sem=sem, src=a, dst=b)
                            for k, (d, sem, a, b) in enumerate(items)], local_sem=S.sloc)
        sent[0] += n * len(items)

    SE, SL = (S.sE0, S.sE1), (S.sL0, S.sL1)
    g.wait_ge(S.sx, 16)
    nv = NV // 2
    g.remote_dma_fused([RemoteDMATransfer(dst_ids=[dst_id(other)], dma_engine_mask=_bits(es_on[k * nv:(k + 1) * nv]),
                                          remote_sem=S.sv, src=T.xs[:, 7 * k, :, :], dst=T.vb[:, k, :, :])
                        for k in range(2)], local_sem=S.sloc)
    sent[0] += NV
    if fs:
        lo, hi = 8 * min(fs), 8 * max(fs) + 8
        g.wait_ge(S.sgb, len(fs))
        call([(other, S.sc, T.cb[:, lo:hi, :, :], T.sb[:, 2 + lo:2 + hi, :, :])])
        lo, hi = 2 * min(fs), 2 * max(fs) + 2
        g.wait_ge(S.sg4, len(fs))
        call([(other, S.sc4, T.c4[:, lo:hi, :, :], T.s4[:, lo:hi, :, :])])
    if rs or ds:
        g.wait_ge(S.sge, len(rs) + len(ds))
    if rs:
        call([(nbr[s][row], SE[1 - s], T.eb[:, s, :, :, :], T.hD[:, 1 - s, 0, :, :, :]) for s in rs])
    for s in ds:
        call([(nbr[s][q], SE[1 - s], T.eb[:, s, :, :, :], T.hD[:, 1 - s, 0 if q == row else 1, :, :, :])
              for q in range(GR)])
    if rs:
        g.wait_ge(S.sgr, len(rs))
        g.wait_ge(S.sc, NO)
        call([(nbr[s][1 - row], SL[1 - s], T.sb[:, 10 * s:10 * s + 10, :, :], T.hA[:, 1 - s, :, :, :]) for s in rs])
        g.wait_ge(S.sc4, NO)
        for s in sorted(rs, key=lambda s: -links(core, nbr[s][row])):
            call([(nbr[s][row], SL[1 - s], T.s4[:, 2 * s:2 * s + 2, :, :], T.hB[:, 1 - s, :, :, :])])
    g.wait_ge(S.sloc, sent[0])

    def wt(a, b):
        t = 3 * a + b
        return T.wsb[:, 128 * t:128 * t + 128]

    n0 = 15
    done = [0]

    def mm0(out, lhsT, rhs):
        done[0] += 1
        g.tensor.matmul(out=out, lhsT=lhsT, rhs=rhs, start=(done[0] == 1), stop=(done[0] == n0)).then_inc(S.sm0, 1)

    out_q = ((1, 8), (0, 8), (0, 7))
    in_c = ((0, 14), (0, 16), (2, 16))
    g.tensor.wait_ge(S.sx, 16)
    for a in (1, 0, 2):
        g.tensor.wait_ge(S["sw%d" % a], 16)
        r0, r1 = ((2, 16), (0, 16), (0, 14))[a]
        p0, p1 = ((0, 7), (0, 8), (1, 8))[a]
        for b in (1, 0, 2):
            mm0(T.p0[:, r0:r1, out_q[b][0]:out_q[b][1], :], wt(a, b), T.xs[:, p0:p1, :, in_c[b][0]:in_c[b][1]])
    g.tensor.wait_ge(S.sv, NV)
    for a in (0, 2):
        r0 = 0 if a == 0 else 14
        k = 1 if a == 0 else 0
        for b in range(3):
            mm0(T.p0[:, r0:r0 + 2, out_q[b][0]:out_q[b][1], :], wt(a, b), T.vb[:, k, :, in_c[b][0]:in_c[b][1]])

    P16 = ((1, 0, 16, 0, 8), (0, 2, 16, 0, 7), (2, 0, 14, 1, 8))
    P4_OF_16 = ((0, 0, 2, 7, 8), (2, 14, 16, 0, 1))
    P4 = ((0, 0, 2, 1, 2), (2, 14, 16, 0, 1))
    PA = (((1, 0, 16, 0, 8), (2, 0, 16, 1, 9), (0, 2, 16, 0, 7), (0, 0, 2, 9, 10)),
          ((1, 0, 16, 2, 10), (0, 0, 16, 1, 9), (2, 0, 14, 3, 10), (2, 14, 16, 0, 1)))
    PE, SME = (T.pe0, T.pe1), (S.sme0, S.sme1)
    early, late, total = [], [], [0, 0]
    for s in range(2):
        k = col - 1 + 2 * s
        rel = relay_of(k, 1 - s)
        if rel is None:
            early.append((0, s, SE[s], NO, [(T.hD[:, s, 0, :, :, :], P16), (T.hD[:, s, 1, :, :, :], P4_OF_16)]))
            total[s] = 5
        elif column(k).index(rel) == row:
            early.append((1, s, SE[s], NO // n_relayed(k), [(T.hD[:, s, 0, :, :, :], P16)]))
            late.append(((1, n_relayed(k), links(rel, core)), s, SL[s], NO, [(T.hB[:, s, :, :, :], P4)]))
            total[s] = 5
        else:
            late.append(((0, n_relayed(k), links(rel, core)), s, SL[s], NO // n_relayed(k), [(T.hA[:, s, :, :, :], PA[s])]))
            total[s] = 4
    count = [0, 0]
    order = []
    for _, s, sem, cnt, parts in sorted(early, key=lambda e: e[0]) + sorted(late, key=lambda e: e[0]):
        g.tensor.wait_ge(sem, cnt)
        for buf, pieces in parts:
            for a, r0, r1, p0, p1 in pieces:
                count[s] += 1
                g.tensor.matmul(out=PE[s][:, r0:r1, :], lhsT=wt(a, 2 * s), rhs=buf[:, p0:p1, :, :],
                                start=(count[s] == 1), stop=(count[s] == total[s])).then_inc(SME[s], 1)
        if count[s] == total[s]:
            order.append(s)

    g.vector.wait_ge(S.sm0, n0)
    g.vector.tensor_copy(out=T.te[:], in_=T.p0[:, 0:16, 0:8:7, :]).then_inc(S.sf, 1)
    g.vector.tensor_copy(out=T.ysb[:, :, 1:7, :], in_=T.p0[:, 0:16, 1:7, :]).then_inc(S.sf, 1)
    g.vector.wait_ge(S.sf, 2)
    for s in order:
        g.vector.wait_ge(SME[s], total[s])
        g.vector.tensor_tensor(out=T.ysb[:, :, 7 * s, :], in0=PE[s][:, 0:16, :], in1=T.te[:, :, s, :],
                               op=AluOpType.add).then_inc(S.sf, 1)

    g.sync.wait_ge(S.sf, 4)
    g.sync.dma_start(T.y[:], T.ysb[:]).then_inc(S.sy, 16)
    g.sync.wait_ge(S.sy, 16)
